import numpy as np
import ml_dtypes


def mxq(x, axis, fmt="e4m3"):
    dtype, down = {"e4m3": (ml_dtypes.float8_e4m3fn, 7), "e5m2": (ml_dtypes.float8_e5m2, 14)}[fmt]
    v = np.moveaxis(np.asarray(x, np.float32).astype(ml_dtypes.bfloat16).astype(np.float64), axis, -1)
    blocks = v.reshape(v.shape[:-1] + (-1, 32))
    amax = np.abs(blocks).max(-1, keepdims=True)
    byte = np.maximum(np.where(amax > 0, np.frexp(amax)[1] - 1 + 127, 0) - down, 1)
    scale = np.exp2(byte - 127.0)
    codes = (blocks / scale).astype(np.float32).astype(dtype).astype(np.float64)
    return np.moveaxis((codes * scale).reshape(v.shape), -1, axis)


WIDE = False


def mx_kscale(k):
    if not WIDE:
        return np.ones(k)
    levels = np.array([10, -10, 5, -5, 0])
    if k % 512:
        return np.exp2(np.random.permutation(np.resize(levels, k // 32))).repeat(32)
    a = np.empty((k // 512, 16))
    for p in range(k // 512):
        a[p, :8] = np.random.permutation(np.resize(levels, 8))
        for g in range(8):
            far = levels[np.abs(levels - a[p, g]) >= 10]
            a[p, g + 8] = far[np.random.randint(len(far))]
    return np.exp2(a.ravel()).repeat(32)


def f64(x):
    return np.asarray(x).astype(np.float64)


def striped(idx):
    return np.tile(np.asarray(idx).reshape(-1, 16).T, (8, 1)).astype(np.uint16)


def unstriped(offs):
    return offs[:16].T.reshape(-1).astype(np.int64)


E2M1 = np.array([0.0, 0.5, 1.0, 1.5, 2.0, 3.0, 4.0, 6.0, -0.0, -0.5, -1.0, -1.5, -2.0, -3.0, -4.0, -6.0])


def pack_weight(w, fmt):
    k, n = w.shape
    w = f64(np.asarray(w, np.float32).astype(ml_dtypes.bfloat16)).reshape(k // 32, 32, n)
    amax = np.abs(w).max(1)
    if fmt == "e4m3":
        byte = np.frexp(amax)[1] - 1 + 127 - 7
    else:
        mant, ex = np.frexp(amax / 6.0)
        byte = np.where(mant > 0.5, ex, ex - 1) + 127
    byte = np.clip(np.where(amax > 0, byte, 1), 1, 254)
    scaled = (w * np.exp2(127.0 - byte)[:, None, :]).reshape(k, n).astype(np.float32)
    by_word = np.ascontiguousarray(scaled.reshape(k // 512, 128, 4, n).transpose(0, 1, 3, 2))
    if fmt == "e4m3":
        words = by_word.astype(ml_dtypes.float8_e4m3fn).view(np.uint8)
    else:
        c = by_word.astype(ml_dtypes.float4_e2m1fn).view(np.uint8) & 0xF
        words = (c[..., 0::2] | (c[..., 1::2] << 4)).reshape(k // 512, 128, 2 * n)
    return np.ascontiguousarray(words), np.ascontiguousarray(byte.astype(np.uint8).reshape(k // 512, 16, n))


def unpack_weight(words, scales, fmt):
    g, _, n = scales.shape
    words = np.ascontiguousarray(words).reshape(g, 128, n, -1)
    if fmt == "e4m3":
        vals = words.view(ml_dtypes.float8_e4m3fn).astype(np.float64)
    else:
        nib = np.empty((g, 128, n, 4), np.uint8)
        nib[..., 0::2] = words & 0xF
        nib[..., 1::2] = words >> 4
        vals = E2M1[nib]
    vals = vals * np.repeat(np.exp2(scales.astype(np.float64) - 127.0), 8, axis=1)[..., None]
    return vals.transpose(0, 1, 3, 2).reshape(g * 512, n)


D, T, U, I, J, G = 512, 1024, 1024, 256, 512, 32


def setup_inputs():
    n = np.random.standard_normal
    idx = np.random.permutation(T)[:I]
    idx2 = np.random.permutation(U)[:J]
    fd = mx_kscale(D)
    tabbp = pack_weight(n((D, U)) / fd[:, None], "e2m1")
    return {
        "taba": (n((D, T)) * 1 / np.sqrt(D) * fd[:, None]).astype(np.float32),
        "dtab": (n((D, T)) * 1.3 / np.sqrt(D) * fd[:, None]).astype(np.float32),
        "tabb_words": tabbp[0],
        "tabb_scales": tabbp[1],
        "aim": (np.random.uniform(0.3, 2.0, (I, G))).astype(np.float32),
        "base": (0.3 * n((I, J))).astype(np.float32),
        "offs": striped(idx),
        "offs2": striped(idx2),
    }


def reference(taba, dtab, tabb_words, tabb_scales, aim, base, offs, offs2):
    idx = unstriped(offs)
    idx2 = unstriped(offs2)
    tabbu = unpack_weight(tabb_words, tabb_scales, "e2m1")
    tabaidxq = mxq(f64(taba)[:, idx], 0, "e4m3")
    tabbidx2g = tabbu[:, idx2]
    s = tabaidxq.T @ tabbidx2g
    dtabidxq = mxq(f64(dtab)[:, idx], 0, "e4m3")
    ts = dtabidxq.T @ tabbidx2g
    v1 = np.sqrt(np.square(s).reshape(I, G, J // G).mean(axis=2) + 0.05)
    dv1 = (v1 - f64(aim)) * 2.0
    e1 = dv1 * 0.5 / np.sqrt(np.square(s).reshape(I, G, J // G).mean(axis=2) + 0.05) / 16.0
    r1 = np.repeat(e1, J // G, axis=1)
    xv1 = (ts * s * 2.0).reshape(I, G, J // G).mean(axis=2) * 0.5 / v1
    xdv1 = xv1 * 2.0
    xe1 = (xdv1 * 0.5 - (ts * s * 2.0).reshape(I, G, J // G).mean(axis=2) * 0.5 / np.sqrt(np.square(s).reshape(I, G, J // G).mean(axis=2) + 0.05) * dv1 * 0.5 / np.sqrt(np.square(s).reshape(I, G, J // G).mean(axis=2) + 0.05)) / np.sqrt(np.square(s).reshape(I, G, J // G).mean(axis=2) + 0.05) / 16.0
    xr1 = np.repeat(xe1, J // G, axis=1)
    xds = (xr1 * s + ts * r1) * 2.0
    y = xds * 8.0 + f64(base)
    return y

@@ -1,0 +1,164 @@
+from contextlib import ExitStack
+
+import concourse.mybir as mybir
+
+D, T, U, I, J, G = 512, 1024, 1024, 256, 512, 32
+P = 128
+PACK = 4
+ROW_TILES = I // P
+GROUP = J // G
+FLOPS = 2 * 2 * D * I * J
+
+F32 = mybir.dt.float32
+BF16 = mybir.dt.bfloat16
+I32 = mybir.dt.int32
+U32 = mybir.dt.uint32
+U16 = mybir.dt.uint16
+U8 = mybir.dt.uint8
+FP8X4 = mybir.dt.float8_e4m3fn_x4
+FP4X4 = mybir.dt.float4_e2m1fn_x4
+ACT = mybir.ActivationFunctionType
+ALU = mybir.AluOpType
+AXIS_X = mybir.AxisListType.X
+
+
+def tile_attend_hvgroupspread_kernel(tc, taba, dtab, tabb_words, tabb_scales, aim, base, offs, offs2, out):
+    nc = tc.nc
+    with ExitStack() as ctx:
+        keep = ctx.enter_context(tc.tile_pool(name="keep", bufs=1))
+        psum = ctx.enter_context(tc.psum_pool(name="psum", bufs=1))
+
+        def sb(shape, dtype, name):
+            return keep.tile(shape, dtype, name=name, align_bytes=64)
+
+        offs_sb = sb([P, I // 16], U16, "offs_sb")
+        offs2_sb = sb([P, J // 16], U16, "offs2_sb")
+        words = sb([P, U], U16, "words")
+        scales = sb([P, U], U8, "scales")
+        a_planes = [sb([P, T], F32, "a_plane%d" % t) for t in range(PACK)]
+        d_planes = [sb([P, T], F32, "d_plane%d" % t) for t in range(PACK)]
+        aim_sb = sb([P, ROW_TILES, G], F32, "aim_sb")
+        base_sb = [sb([P, J], F32, "base_sb%d" % c) for c in range(ROW_TILES)]
+
+        nc.vector.memset(scales[:].bitcast(I32), 0)
+        one = sb([P, 2], F32, "one")
+        nc.vector.memset(one[:], 1.0)
+        nc.sync.dma_start(offs2_sb[:], offs2)
+        nc.sync.dma_start(out=words[:].bitcast(I32), in_=tabb_words[0].bitcast(I32))
+        a_rows = taba.rearrange("(p t) c -> t p c", t=PACK)
+        d_rows = dtab.rearrange("(p t) c -> t p c", t=PACK)
+        nc.sync.dma_start(out=a_planes[0][:], in_=a_rows[0])
+        for q in range(4):
+            nc.sync.dma_start(
+                out=scales[32 * q : 32 * q + 4, :].bitcast(I32),
+                in_=tabb_scales[0, 4 * q : 4 * q + 4, :].bitcast(I32),
+            )
+        nc.sync.dma_start(out=a_planes[1][:], in_=a_rows[1])
+        nc.sync.dma_start(offs_sb[:], offs)
+        for t in (2, 3):
+            nc.sync.dma_start(out=a_planes[t][:], in_=a_rows[t])
+        for t in range(PACK):
+            nc.sync.dma_start(out=d_planes[t][:], in_=d_rows[t])
+        nc.sync.dma_start(out=aim_sb[:], in_=aim.rearrange("(c p) g -> p c g", p=P))
+        for c in range(ROW_TILES):
+            nc.sync.dma_start(out=base_sb[c][:], in_=base[c * P : (c + 1) * P, :])
+
+        warm = sb([P, 2], F32, "warm")
+        nc.scalar.activation(warm[:], one[:], ACT.Abs_reciprocal_sqrt)
+
+        b_words = sb([P, J], U16, "b_words")
+        b_scales = sb([P, J], U8, "b_scales")
+        nc.vector.tensor_copy(b_words[:], words[:].indirect(offs2_sb[:]))
+        nc.vector.tensor_copy(b_scales[:], scales[:].indirect(offs2_sb[:]))
+
+        a_woven = sb([P, I, PACK], BF16, "a_woven")
+        for t in (0, 1):
+            a_cast = sb([P, T], BF16, "a_cast%d" % t)
+            nc.scalar.activation(a_cast[:], a_planes[t][:], ACT.Copy)
+            nc.scalar.activation(a_woven[:, :, t], a_cast[:].indirect(offs_sb[:]), ACT.Copy)
+        for t in (2, 3):
+            nc.vector.tensor_copy(a_woven[:, :, t], a_planes[t][:].indirect(offs_sb[:]))
+
+        def scores(woven, c, name):
+            codes = sb([P, P], U32, name + "_codes")
+            plane = sb([P, P], U8, name + "_plane")
+            nc.vector.quantize_mx(
+                out=codes[:].bitcast(FP8X4),
+                scales=plane[:],
+                in_=woven[:, c * P : (c + 1) * P, :].rearrange("p i t -> p (i t)"),
+            )
+            bank = psum.tile([P, J], F32, name=name)
+            nc.tensor.matmul_mx(
+                out=bank[:],
+                lhsT=codes[:].bitcast(FP8X4),
+                lhsT_scale=plane[:],
+                rhs=b_words[:].bitcast(FP4X4),
+                rhs_scale=b_scales[:],
+                start=True,
+                stop=True,
+            )
+            return bank
+
+        def grouped(bank):
+            return bank[:].rearrange("p (g r) -> p g r", r=GROUP)
+
+        s = [scores(a_woven, c, "s%d" % c) for c in range(ROW_TILES)]
+        d_woven = sb([P, I, PACK], BF16, "a_woven")
+        for t in range(PACK - 1):
+            nc.vector.tensor_copy(d_woven[:, :, t], d_planes[t][:].indirect(offs_sb[:]))
+
+        sum_sq = sb([P, ROW_TILES, G], F32, "d_plane1")
+        for c in range(ROW_TILES):
+            sq = sb([P, G, GROUP], F32, "sq%d" % c)
+            nc.scalar.activation(sq[:], grouped(s[c]), ACT.Square)
+            nc.vector.tensor_reduce(sum_sq[:, c, :], sq[:], AXIS_X, ALU.add)
+
+        inv_v = sb([P, ROW_TILES, G], F32, "inv_v")
+        nc.scalar.activation(inv_v[:], sum_sq[:], ACT.Abs_reciprocal_sqrt, bias=0.05, scale=1.0 / GROUP)
+        inv_v2 = sb([P, ROW_TILES, G], F32, "inv_v2")
+        nc.scalar.activation(inv_v2[:], inv_v[:], ACT.Square, scale=0.25)
+        ratio = sb([P, ROW_TILES, G], F32, "ratio")
+        nc.gpsimd.tensor_tensor(ratio[:], aim_sb[:], inv_v[:], ALU.mult)
+        curv = sb([P, ROW_TILES, G], F32, "curv")
+        nc.gpsimd.tensor_tensor(curv[:], ratio[:], inv_v2[:], ALU.mult)
+        s_sb = []
+        for c in range(ROW_TILES):
+            s_sb.append(sb([P, G, GROUP], F32, "s_sb%d" % c))
+            nc.scalar.copy(s_sb[c][:], grouped(s[c]))
+
+        ts = []
+        for c in range(ROW_TILES):
+            rows = slice(c * P, (c + 1) * P)
+            nc.vector.tensor_copy(d_woven[:, rows, 3], d_planes[3][:].indirect(offs_sb[:, 8 * c : 8 * (c + 1)]))
+            ts.append(scores(d_woven, c, "ts%d" % c))
+
+        def spread(x, width):
+            return x.unsqueeze(2).to_broadcast([P, G, width])
+
+        prod = []
+        partial = []
+        for c in range(ROW_TILES):
+            prod.append(sb([P, G, GROUP], F32, "prod%d" % c))
+            nc.vector.tensor_tensor(prod[c][:], grouped(ts[c]), s_sb[c][:], ALU.mult)
+            term = sb([P, J], F32, "term%d" % c)
+            nc.vector.scalar_tensor_tensor(
+                grouped(term), spread(ratio[:, c, :], GROUP), 1.0, grouped(ts[c]), ALU.subtract, ALU.mult
+            )
+            partial.append(sb([P, J], F32, "partial%d" % c))
+            nc.gpsimd.tensor_tensor(partial[c][:], base_sb[c][:], term[:], ALU.subtract)
+        dots = []
+        for c in range(ROW_TILES):
+            dots.append(sb([P, G], F32, "dots%d" % c))
+            nc.vector.tensor_reduce(dots[c][:], prod[c][:], AXIS_X, ALU.add)
+        f_s = []
+        for c in range(ROW_TILES):
+            f_s.append(sb([P, G], F32, "f_s%d" % c))
+            nc.vector.tensor_tensor(f_s[c][:], dots[c][:], curv[:, c, :], ALU.mult)
+        along = []
+        for c in range(ROW_TILES):
+            along.append(sb([P, J], F32, "along%d" % c))
+            nc.vector.tensor_tensor(grouped(along[c]), grouped(s[c]), spread(f_s[c][:], GROUP), ALU.mult)
+        for c in range(ROW_TILES):
+            result = sb([P, J], F32, "result%d" % c)
+            nc.vector.tensor_tensor(result[:], along[c][:], partial[c][:], ALU.add)
+            nc.sync.dma_start(out=out[c * P : (c + 1) * P, :], in_=result[:])

@@ -71,21 +71,29 @@ def tile_attend_hvgroupspread_kernel(tc, taba, dtab, tabb_words, tabb_scales, ai
         nc.vector.tensor_copy(b_words[:], words[:].indirect(offs2_sb[:]))
         nc.vector.tensor_copy(b_scales[:], scales[:].indirect(offs2_sb[:]))
 
-        a_woven = sb([P, I, PACK], BF16, "a_woven")
+        a_flat = sb([P, PACK, I], BF16, "a_flat")
         for t in (0, 1):
             a_cast = sb([P, T], BF16, "a_cast%d" % t)
             nc.scalar.activation(a_cast[:], a_planes[t][:], ACT.Copy)
-            nc.scalar.activation(a_woven[:, :, t], a_cast[:].indirect(offs_sb[:]), ACT.Copy)
+            nc.scalar.activation(a_flat[:, t, :], a_cast[:].indirect(offs_sb[:]), ACT.Copy)
         for t in (2, 3):
-            nc.vector.tensor_copy(a_woven[:, :, t], a_planes[t][:].indirect(offs_sb[:]))
+            nc.vector.tensor_copy(a_flat[:, t, :], a_planes[t][:].indirect(offs_sb[:]))
 
-        def scores(woven, c, name):
+        def weave(copy, flat, c, name):
+            woven = sb([P, P, PACK], BF16, name + "_woven")
+            copy(
+                woven[:].rearrange("p (q i) t -> p q t i", i=4),
+                flat[:, :, c * P : (c + 1) * P].rearrange("p t (q i) -> p q t i", i=4),
+            )
+            return woven
+
+        def scores(woven, name):
             codes = sb([P, P], U32, name + "_codes")
             plane = sb([P, P], U8, name + "_plane")
             nc.vector.quantize_mx(
                 out=codes[:].bitcast(FP8X4),
                 scales=plane[:],
-                in_=woven[:, c * P : (c + 1) * P, :].rearrange("p i t -> p (i t)"),
+                in_=woven[:].rearrange("p i t -> p (i t)"),
             )
             bank = psum.tile([P, J], F32, name=name)
             nc.tensor.matmul_mx(
@@ -102,35 +110,42 @@ def tile_attend_hvgroupspread_kernel(tc, taba, dtab, tabb_words, tabb_scales, ai
         def grouped(bank):
             return bank[:].rearrange("p (g r) -> p g r", r=GROUP)
 
-        s = [scores(a_woven, c, "s%d" % c) for c in range(ROW_TILES)]
-        d_woven = sb([P, I, PACK], BF16, "a_woven")
+        a_woven = [weave(nc.scalar.copy, a_flat, c, "s%d" % c) for c in range(ROW_TILES)]
+        s = [scores(a_woven[c], "s%d" % c) for c in range(ROW_TILES)]
+        d_flat = sb([P, PACK, I], BF16, "d_flat")
         for t in range(PACK - 1):
-            nc.vector.tensor_copy(d_woven[:, :, t], d_planes[t][:].indirect(offs_sb[:]))
+            nc.vector.tensor_copy(d_flat[:, t, :], d_planes[t][:].indirect(offs_sb[:]))
 
-        sum_sq = sb([P, ROW_TILES, G], F32, "d_plane1")
-        for c in range(ROW_TILES):
-            sq = sb([P, G, GROUP], F32, "sq%d" % c)
-            nc.scalar.activation(sq[:], grouped(s[c]), ACT.Square)
-            nc.vector.tensor_reduce(sum_sq[:, c, :], sq[:], AXIS_X, ALU.add)
-
-        inv_v = sb([P, ROW_TILES, G], F32, "inv_v")
-        nc.scalar.activation(inv_v[:], sum_sq[:], ACT.Abs_reciprocal_sqrt, bias=0.05, scale=1.0 / GROUP)
-        inv_v2 = sb([P, ROW_TILES, G], F32, "inv_v2")
-        nc.scalar.activation(inv_v2[:], inv_v[:], ACT.Square, scale=0.25)
-        ratio = sb([P, ROW_TILES, G], F32, "ratio")
-        nc.gpsimd.tensor_tensor(ratio[:], aim_sb[:], inv_v[:], ALU.mult)
-        curv = sb([P, ROW_TILES, G], F32, "curv")
-        nc.gpsimd.tensor_tensor(curv[:], ratio[:], inv_v2[:], ALU.mult)
+        sq = []
         s_sb = []
+        for c in range(ROW_TILES):
+            sq.append(sb([P, G, GROUP], F32, "sq%d" % c))
+            nc.scalar.activation(sq[c][:], grouped(s[c]), ACT.Square)
         for c in range(ROW_TILES):
             s_sb.append(sb([P, G, GROUP], F32, "s_sb%d" % c))
             nc.scalar.copy(s_sb[c][:], grouped(s[c]))
 
-        ts = []
+        def factors(c, slot):
+            sum_sq = sb([P, G], F32, slot)
+            nc.vector.tensor_reduce(sum_sq[:], sq[c][:], AXIS_X, ALU.add)
+            inv_v = sb([P, G], F32, "inv_v%d" % c)
+            nc.scalar.activation(inv_v[:], sum_sq[:], ACT.Abs_reciprocal_sqrt, bias=0.05, scale=1.0 / GROUP)
+            inv_v2 = sb([P, G], F32, "inv_v2_%d" % c)
+            nc.scalar.activation(inv_v2[:], inv_v[:], ACT.Square, scale=0.25)
+            nc.gpsimd.tensor_tensor(ratio[:, c, :], aim_sb[:, c, :], inv_v[:], ALU.mult)
+            nc.gpsimd.tensor_tensor(curv[:, c, :], ratio[:, c, :], inv_v2[:], ALU.mult)
+
+        ratio = sb([P, ROW_TILES, G], F32, "ratio")
+        curv = sb([P, ROW_TILES, G], F32, "curv")
+        factors(0, "d_plane2")
         for c in range(ROW_TILES):
-            rows = slice(c * P, (c + 1) * P)
-            nc.vector.tensor_copy(d_woven[:, rows, 3], d_planes[3][:].indirect(offs_sb[:, 8 * c : 8 * (c + 1)]))
-            ts.append(scores(d_woven, c, "ts%d" % c))
+            nc.vector.tensor_copy(
+                d_flat[:, PACK - 1, c * P : (c + 1) * P],
+                d_planes[PACK - 1][:].indirect(offs_sb[:, 8 * c : 8 * (c + 1)]),
+            )
+        d_woven = [weave(nc.vector.tensor_copy, d_flat, c, "ts%d" % c) for c in range(ROW_TILES)]
+        ts = [scores(d_woven[c], "ts%d" % c) for c in range(ROW_TILES)]
+        factors(1, "ts1_woven")
 
         def spread(x, width):
             return x.unsqueeze(2).to_broadcast([P, G, width])
@@ -158,7 +173,9 @@ def tile_attend_hvgroupspread_kernel(tc, taba, dtab, tabb_words, tabb_scales, ai
         for c in range(ROW_TILES):
             along.append(sb([P, J], F32, "along%d" % c))
             nc.vector.tensor_tensor(grouped(along[c]), grouped(s[c]), spread(f_s[c][:], GROUP), ALU.mult)
-        for c in range(ROW_TILES):
-            result = sb([P, J], F32, "result%d" % c)
-            nc.vector.tensor_tensor(result[:], along[c][:], partial[c][:], ALU.add)
-            nc.sync.dma_start(out=out[c * P : (c + 1) * P, :], in_=result[:])
+        half = J // 2
+        pieces = [(0, slice(0, J), nc.sync), (1, slice(0, half), nc.scalar), (1, slice(half, J), nc.sync)]
+        for n, (c, cols, queue) in enumerate(pieces):
+            result = sb([P, cols.stop - cols.start], F32, "result%d" % n)
+            nc.vector.tensor_tensor(result[:], along[c][:, cols], partial[c][:, cols], ALU.add)
+            queue.dma_start(out=out[c * P : (c + 1) * P, cols], in_=result[:])

@@ -44,17 +44,17 @@ def tile_attend_hvgroupspread_kernel(tc, taba, dtab, tabb_words, tabb_scales, ai
         one = sb([P, 2], F32, "one")
         nc.vector.memset(one[:], 1.0)
         nc.sync.dma_start(offs2_sb[:], offs2)
+        nc.sync.dma_start(offs_sb[:], offs)
         nc.sync.dma_start(out=words[:].bitcast(I32), in_=tabb_words[0].bitcast(I32))
         a_rows = taba.rearrange("(p t) c -> t p c", t=PACK)
         d_rows = dtab.rearrange("(p t) c -> t p c", t=PACK)
-        nc.sync.dma_start(out=a_planes[0][:], in_=a_rows[0])
+        for t in (0, 1):
+            nc.sync.dma_start(out=a_planes[t][:], in_=a_rows[t])
         for q in range(4):
             nc.sync.dma_start(
                 out=scales[32 * q : 32 * q + 4, :].bitcast(I32),
                 in_=tabb_scales[0, 4 * q : 4 * q + 4, :].bitcast(I32),
             )
-        nc.sync.dma_start(out=a_planes[1][:], in_=a_rows[1])
-        nc.sync.dma_start(offs_sb[:], offs)
         for t in (2, 3):
             nc.sync.dma_start(out=a_planes[t][:], in_=a_rows[t])
         for t in range(PACK):
@@ -125,19 +125,23 @@ def tile_attend_hvgroupspread_kernel(tc, taba, dtab, tabb_words, tabb_scales, ai
             s_sb.append(sb([P, G, GROUP], F32, "s_sb%d" % c))
             nc.scalar.copy(s_sb[c][:], grouped(s[c]))
 
-        def factors(c, slot):
+        def inverse_spread(c, slot):
             sum_sq = sb([P, G], F32, slot)
             nc.vector.tensor_reduce(sum_sq[:], sq[c][:], AXIS_X, ALU.add)
             inv_v = sb([P, G], F32, "inv_v%d" % c)
             nc.scalar.activation(inv_v[:], sum_sq[:], ACT.Abs_reciprocal_sqrt, bias=0.05, scale=1.0 / GROUP)
             inv_v2 = sb([P, G], F32, "inv_v2_%d" % c)
             nc.scalar.activation(inv_v2[:], inv_v[:], ACT.Square, scale=0.25)
-            nc.gpsimd.tensor_tensor(ratio[:, c, :], aim_sb[:, c, :], inv_v[:], ALU.mult)
-            nc.gpsimd.tensor_tensor(curv[:, c, :], ratio[:, c, :], inv_v2[:], ALU.mult)
+            return inv_v, inv_v2
 
-        ratio = sb([P, ROW_TILES, G], F32, "ratio")
-        curv = sb([P, ROW_TILES, G], F32, "curv")
-        factors(0, "d_plane2")
+        def factors(c, inv_v, inv_v2, slot):
+            ratio_c = sb([P, G], F32, slot)
+            nc.gpsimd.tensor_tensor(ratio_c[:], aim_sb[:, c, :], inv_v[:], ALU.mult)
+            curv_c = sb([P, G], F32, "curv%d" % c)
+            nc.gpsimd.tensor_tensor(curv_c[:], ratio_c[:], inv_v2[:], ALU.mult)
+            return ratio_c, curv_c
+
+        inverse = [inverse_spread(0, "d_plane2")]
         for c in range(ROW_TILES):
             nc.vector.tensor_copy(
                 d_flat[:, PACK - 1, c * P : (c + 1) * P],
@@ -145,7 +149,8 @@ def tile_attend_hvgroupspread_kernel(tc, taba, dtab, tabb_words, tabb_scales, ai
             )
         d_woven = [weave(nc.vector.tensor_copy, d_flat, c, "ts%d" % c) for c in range(ROW_TILES)]
         ts = [scores(d_woven[c], "ts%d" % c) for c in range(ROW_TILES)]
-        factors(1, "ts1_woven")
+        inverse.append(inverse_spread(1, "ts0_woven"))
+        ratio, curv = zip(factors(0, *inverse[0], "ts1_woven"), factors(1, *inverse[1], "ratio1"))
 
         def spread(x, width):
             return x.unsqueeze(2).to_broadcast([P, G, width])
@@ -153,14 +158,14 @@ def tile_attend_hvgroupspread_kernel(tc, taba, dtab, tabb_words, tabb_scales, ai
         prod = []
         partial = []
         for c in range(ROW_TILES):
-            prod.append(sb([P, G, GROUP], F32, "prod%d" % c))
-            nc.vector.tensor_tensor(prod[c][:], grouped(ts[c]), s_sb[c][:], ALU.mult)
             term = sb([P, J], F32, "term%d" % c)
             nc.vector.scalar_tensor_tensor(
-                grouped(term), spread(ratio[:, c, :], GROUP), 1.0, grouped(ts[c]), ALU.subtract, ALU.mult
+                grouped(term), spread(ratio[c][:], GROUP), 1.0, grouped(ts[c]), ALU.subtract, ALU.mult
             )
             partial.append(sb([P, J], F32, "partial%d" % c))
             nc.gpsimd.tensor_tensor(partial[c][:], base_sb[c][:], term[:], ALU.subtract)
+            prod.append(sb([P, G, GROUP], F32, "prod%d" % c))
+            nc.vector.tensor_tensor(prod[c][:], grouped(ts[c]), s_sb[c][:], ALU.mult)
         dots = []
         for c in range(ROW_TILES):
             dots.append(sb([P, G], F32, "dots%d" % c))
@@ -168,7 +173,7 @@ def tile_attend_hvgroupspread_kernel(tc, taba, dtab, tabb_words, tabb_scales, ai
         f_s = []
         for c in range(ROW_TILES):
             f_s.append(sb([P, G], F32, "f_s%d" % c))
-            nc.vector.tensor_tensor(f_s[c][:], dots[c][:], curv[:, c, :], ALU.mult)
+            nc.vector.tensor_tensor(f_s[c][:], dots[c][:], curv[c][:], ALU.mult)
         along = []
         for c in range(ROW_TILES):
             along.append(sb([P, J], F32, "along%d" % c))

@@ -79,9 +79,9 @@ def tile_attend_hvgroupspread_kernel(tc, taba, dtab, tabb_words, tabb_scales, ai
         for t in (2, 3):
             nc.vector.tensor_copy(a_flat[:, t, :], a_planes[t][:].indirect(offs_sb[:]))
 
-        def weave(copy, flat, c, name):
+        def weave(flat, c, name):
             woven = sb([P, P, PACK], BF16, name + "_woven")
-            copy(
+            nc.scalar.copy(
                 woven[:].rearrange("p (q i) t -> p q t i", i=4),
                 flat[:, :, c * P : (c + 1) * P].rearrange("p t (q i) -> p q t i", i=4),
             )
@@ -93,7 +93,7 @@ def tile_attend_hvgroupspread_kernel(tc, taba, dtab, tabb_words, tabb_scales, ai
             nc.vector.quantize_mx(
                 out=codes[:].bitcast(FP8X4),
                 scales=plane[:],
-                in_=woven[:].rearrange("p i t -> p (i t)"),
+                in_=woven.rearrange("p i t -> p (i t)"),
             )
             bank = psum.tile([P, J], F32, name=name)
             nc.tensor.matmul_mx(
@@ -110,17 +110,23 @@ def tile_attend_hvgroupspread_kernel(tc, taba, dtab, tabb_words, tabb_scales, ai
         def grouped(bank):
             return bank[:].rearrange("p (g r) -> p g r", r=GROUP)
 
-        a_woven = [weave(nc.scalar.copy, a_flat, c, "s%d" % c) for c in range(ROW_TILES)]
-        s = [scores(a_woven[c], "s%d" % c) for c in range(ROW_TILES)]
-        d_flat = sb([P, PACK, I], BF16, "d_flat")
-        for t in range(PACK - 1):
+        a_woven = [weave(a_flat, c, "s%d" % c) for c in range(ROW_TILES)]
+        s = [scores(a_woven[c][:], "s%d" % c) for c in range(ROW_TILES)]
+        d_flat = sb([P, 2, I], BF16, "d_flat")
+        d_woven = sb([P, I, PACK], BF16, "d_woven")
+        for t in (0, 1):
             nc.vector.tensor_copy(d_flat[:, t, :], d_planes[t][:].indirect(offs_sb[:]))
+        nc.vector.tensor_copy(d_woven[:, :, 2], d_planes[2][:].indirect(offs_sb[:]))
 
         sq = []
         s_sb = []
         for c in range(ROW_TILES):
             sq.append(sb([P, G, GROUP], F32, "sq%d" % c))
             nc.scalar.activation(sq[c][:], grouped(s[c]), ACT.Square)
+        nc.scalar.copy(
+            d_woven[:, :, 0:2].rearrange("p (q i) t -> p q t i", i=4),
+            d_flat[:].rearrange("p t (q i) -> p q t i", i=4),
+        )
         for c in range(ROW_TILES):
             s_sb.append(sb([P, G, GROUP], F32, "s_sb%d" % c))
             nc.scalar.copy(s_sb[c][:], grouped(s[c]))
@@ -144,13 +150,12 @@ def tile_attend_hvgroupspread_kernel(tc, taba, dtab, tabb_words, tabb_scales, ai
         inverse = [inverse_spread(0, "d_plane2")]
         for c in range(ROW_TILES):
             nc.vector.tensor_copy(
-                d_flat[:, PACK - 1, c * P : (c + 1) * P],
+                d_woven[:, c * P : (c + 1) * P, PACK - 1],
                 d_planes[PACK - 1][:].indirect(offs_sb[:, 8 * c : 8 * (c + 1)]),
             )
-        d_woven = [weave(nc.vector.tensor_copy, d_flat, c, "ts%d" % c) for c in range(ROW_TILES)]
-        ts = [scores(d_woven[c], "ts%d" % c) for c in range(ROW_TILES)]
-        inverse.append(inverse_spread(1, "ts0_woven"))
-        ratio, curv = zip(factors(0, *inverse[0], "ts1_woven"), factors(1, *inverse[1], "ratio1"))
+        ts = [scores(d_woven[:, c * P : (c + 1) * P, :], "ts%d" % c) for c in range(ROW_TILES)]
+        inverse.append(inverse_spread(1, "d_plane3"))
+        ratio, curv = zip(factors(0, *inverse[0], "d_woven"), factors(1, *inverse[1], "ratio1"))
 
         def spread(x, width):
             return x.unsqueeze(2).to_broadcast([P, G, width])
@@ -174,13 +179,23 @@ def tile_attend_hvgroupspread_kernel(tc, taba, dtab, tabb_words, tabb_scales, ai
         for c in range(ROW_TILES):
             f_s.append(sb([P, G], F32, "f_s%d" % c))
             nc.vector.tensor_tensor(f_s[c][:], dots[c][:], curv[c][:], ALU.mult)
-        along = []
-        for c in range(ROW_TILES):
-            along.append(sb([P, J], F32, "along%d" % c))
-            nc.vector.tensor_tensor(grouped(along[c]), grouped(s[c]), spread(f_s[c][:], GROUP), ALU.mult)
-        half = J // 2
-        pieces = [(0, slice(0, J), nc.sync), (1, slice(0, half), nc.scalar), (1, slice(half, J), nc.sync)]
-        for n, (c, cols, queue) in enumerate(pieces):
-            result = sb([P, cols.stop - cols.start], F32, "result%d" % n)
+        along = [sb([P, J], F32, "along%d" % c) for c in range(ROW_TILES)]
+
+        def scale_scores(c, groups):
+            n = groups.stop - groups.start
+            factor = f_s[c][:, groups].unsqueeze(2).to_broadcast([P, n, GROUP])
+            nc.vector.tensor_tensor(grouped(along[c])[:, groups, :], grouped(s[c])[:, groups, :], factor, ALU.mult)
+
+        def finish(c, groups, queue):
+            cols = slice(groups.start * GROUP, groups.stop * GROUP)
+            result = sb([P, cols.stop - cols.start], F32, "result%d_%d" % (c, groups.start))
             nc.vector.tensor_tensor(result[:], along[c][:, cols], partial[c][:, cols], ALU.add)
             queue.dma_start(out=out[c * P : (c + 1) * P, cols], in_=result[:])
+
+        whole, low, high = slice(0, G), slice(0, G // 2), slice(G // 2, G)
+        scale_scores(0, whole)
+        scale_scores(1, low)
+        finish(0, whole, nc.sync)
+        scale_scores(1, high)
+        finish(1, low, nc.scalar)
+        finish(1, high, nc.sync)

from contextlib import ExitStack

import concourse.mybir as mybir

D, T, U, I, J, G = 512, 1024, 1024, 256, 512, 32
P = 128
PACK = 4
ROW_TILES = I // P
GROUP = J // G
FLOPS = 2 * 2 * D * I * J

F32 = mybir.dt.float32
BF16 = mybir.dt.bfloat16
I32 = mybir.dt.int32
U32 = mybir.dt.uint32
U16 = mybir.dt.uint16
U8 = mybir.dt.uint8
FP8X4 = mybir.dt.float8_e4m3fn_x4
FP4X4 = mybir.dt.float4_e2m1fn_x4
ACT = mybir.ActivationFunctionType
ALU = mybir.AluOpType
AXIS_X = mybir.AxisListType.X


def tile_attend_hvgroupspread_kernel(tc, taba, dtab, tabb_words, tabb_scales, aim, base, offs, offs2, out):
    nc = tc.nc
    with ExitStack() as ctx:
        keep = ctx.enter_context(tc.tile_pool(name="keep", bufs=1))
        psum = ctx.enter_context(tc.psum_pool(name="psum", bufs=1))

        def sb(shape, dtype, name):
            return keep.tile(shape, dtype, name=name, align_bytes=64)

        offs_sb = sb([P, I // 16], U16, "offs_sb")
        offs2_sb = sb([P, J // 16], U16, "offs2_sb")
        words = sb([P, U], U16, "words")
        scales = sb([P, U], U8, "scales")
        a_planes = [sb([P, T], F32, "a_plane%d" % t) for t in range(PACK)]
        d_planes = [sb([P, T], F32, "d_plane%d" % t) for t in range(PACK)]
        aim_sb = sb([P, ROW_TILES, G], F32, "aim_sb")
        base_sb = [sb([P, J], F32, "base_sb%d" % c) for c in range(ROW_TILES)]

        nc.vector.memset(scales[:].bitcast(I32), 0)
        one = sb([P, 2], F32, "one")
        nc.vector.memset(one[:], 1.0)
        nc.sync.dma_start(offs2_sb[:], offs2)
        nc.sync.dma_start(offs_sb[:], offs)
        nc.sync.dma_start(out=words[:].bitcast(I32), in_=tabb_words[0].bitcast(I32))
        a_rows = taba.rearrange("(p t) c -> t p c", t=PACK)
        d_rows = dtab.rearrange("(p t) c -> t p c", t=PACK)
        for t in (0, 1):
            nc.sync.dma_start(out=a_planes[t][:], in_=a_rows[t])
        for q in range(4):
            nc.sync.dma_start(
                out=scales[32 * q : 32 * q + 4, :].bitcast(I32),
                in_=tabb_scales[0, 4 * q : 4 * q + 4, :].bitcast(I32),
            )
        for t in (2, 3):
            nc.sync.dma_start(out=a_planes[t][:], in_=a_rows[t])
        for t in range(PACK):
            nc.sync.dma_start(out=d_planes[t][:], in_=d_rows[t])
        nc.sync.dma_start(out=aim_sb[:], in_=aim.rearrange("(c p) g -> p c g", p=P))
        for c in range(ROW_TILES):
            nc.sync.dma_start(out=base_sb[c][:], in_=base[c * P : (c + 1) * P, :])

        warm = sb([P, 2], F32, "warm")
        nc.scalar.activation(warm[:], one[:], ACT.Abs_reciprocal_sqrt)

        b_words = sb([P, J], U16, "b_words")
        b_scales = sb([P, J], U8, "b_scales")
        nc.vector.tensor_copy(b_words[:], words[:].indirect(offs2_sb[:]))
        nc.vector.tensor_copy(b_scales[:], scales[:].indirect(offs2_sb[:]))

        a_flat = sb([P, PACK, I], BF16, "a_flat")
        for t in (0, 1):
            a_cast = sb([P, T], BF16, "a_cast%d" % t)
            nc.scalar.activation(a_cast[:], a_planes[t][:], ACT.Copy)
            nc.scalar.activation(a_flat[:, t, :], a_cast[:].indirect(offs_sb[:]), ACT.Copy)
        for t in (2, 3):
            nc.vector.tensor_copy(a_flat[:, t, :], a_planes[t][:].indirect(offs_sb[:]))

        def weave(flat, c, name):
            woven = sb([P, P, PACK], BF16, name + "_woven")
            nc.scalar.copy(
                woven[:].rearrange("p (q i) t -> p q t i", i=4),
                flat[:, :, c * P : (c + 1) * P].rearrange("p t (q i) -> p q t i", i=4),
            )
            return woven

        def scores(woven, name):
            codes = sb([P, P], U32, name + "_codes")
            plane = sb([P, P], U8, name + "_plane")
            nc.vector.quantize_mx(
                out=codes[:].bitcast(FP8X4),
                scales=plane[:],
                in_=woven.rearrange("p i t -> p (i t)"),
            )
            bank = psum.tile([P, J], F32, name=name)
            nc.tensor.matmul_mx(
                out=bank[:],
                lhsT=codes[:].bitcast(FP8X4),
                lhsT_scale=plane[:],
                rhs=b_words[:].bitcast(FP4X4),
                rhs_scale=b_scales[:],
                start=True,
                stop=True,
            )
            return bank

        def grouped(bank):
            return bank[:].rearrange("p (g r) -> p g r", r=GROUP)

        a_woven = [weave(a_flat, c, "s%d" % c) for c in range(ROW_TILES)]
        s = [scores(a_woven[c][:], "s%d" % c) for c in range(ROW_TILES)]
        d_flat = sb([P, 2, I], BF16, "d_flat")
        d_woven = sb([P, I, PACK], BF16, "d_woven")
        for t in (0, 1):
            nc.vector.tensor_copy(d_flat[:, t, :], d_planes[t][:].indirect(offs_sb[:]))
        nc.vector.tensor_copy(d_woven[:, :, 2], d_planes[2][:].indirect(offs_sb[:]))

        sq = []
        s_sb = []
        for c in range(ROW_TILES):
            sq.append(sb([P, G, GROUP], F32, "sq%d" % c))
            nc.scalar.activation(sq[c][:], grouped(s[c]), ACT.Square)
        nc.scalar.copy(
            d_woven[:, :, 0:2].rearrange("p (q i) t -> p q t i", i=4),
            d_flat[:].rearrange("p t (q i) -> p q t i", i=4),
        )
        for c in range(ROW_TILES):
            s_sb.append(sb([P, G, GROUP], F32, "s_sb%d" % c))
            nc.scalar.copy(s_sb[c][:], grouped(s[c]))

        def inverse_spread(c, slot):
            sum_sq = sb([P, G], F32, slot)
            nc.vector.tensor_reduce(sum_sq[:], sq[c][:], AXIS_X, ALU.add)
            inv_v = sb([P, G], F32, "inv_v%d" % c)
            nc.scalar.activation(inv_v[:], sum_sq[:], ACT.Abs_reciprocal_sqrt, bias=0.05, scale=1.0 / GROUP)
            inv_v2 = sb([P, G], F32, "inv_v2_%d" % c)
            nc.scalar.activation(inv_v2[:], inv_v[:], ACT.Square, scale=0.25)
            return inv_v, inv_v2

        def factors(c, inv_v, inv_v2, slot):
            ratio_c = sb([P, G], F32, slot)
            nc.gpsimd.tensor_tensor(ratio_c[:], aim_sb[:, c, :], inv_v[:], ALU.mult)
            curv_c = sb([P, G], F32, "curv%d" % c)
            nc.gpsimd.tensor_tensor(curv_c[:], ratio_c[:], inv_v2[:], ALU.mult)
            return ratio_c, curv_c

        inverse = [inverse_spread(0, "d_plane2")]
        for c in range(ROW_TILES):
            nc.vector.tensor_copy(
                d_woven[:, c * P : (c + 1) * P, PACK - 1],
                d_planes[PACK - 1][:].indirect(offs_sb[:, 8 * c : 8 * (c + 1)]),
            )
        ts = [scores(d_woven[:, c * P : (c + 1) * P, :], "ts%d" % c) for c in range(ROW_TILES)]
        inverse.append(inverse_spread(1, "d_plane3"))
        ratio, curv = zip(factors(0, *inverse[0], "d_woven"), factors(1, *inverse[1], "ratio1"))

        def spread(x, width):
            return x.unsqueeze(2).to_broadcast([P, G, width])

        prod = []
        partial = []
        for c in range(ROW_TILES):
            term = sb([P, J], F32, "term%d" % c)
            nc.vector.scalar_tensor_tensor(
                grouped(term), spread(ratio[c][:], GROUP), 1.0, grouped(ts[c]), ALU.subtract, ALU.mult
            )
            partial.append(sb([P, J], F32, "partial%d" % c))
            nc.gpsimd.tensor_tensor(partial[c][:], base_sb[c][:], term[:], ALU.subtract)
            prod.append(sb([P, G, GROUP], F32, "prod%d" % c))
            nc.vector.tensor_tensor(prod[c][:], grouped(ts[c]), s_sb[c][:], ALU.mult)
        dots = []
        for c in range(ROW_TILES):
            dots.append(sb([P, G], F32, "dots%d" % c))
            nc.vector.tensor_reduce(dots[c][:], prod[c][:], AXIS_X, ALU.add)
        f_s = []
        for c in range(ROW_TILES):
            f_s.append(sb([P, G], F32, "f_s%d" % c))
            nc.vector.tensor_tensor(f_s[c][:], dots[c][:], curv[c][:], ALU.mult)
        along = [sb([P, J], F32, "along%d" % c) for c in range(ROW_TILES)]

        def scale_scores(c, groups):
            n = groups.stop - groups.start
            factor = f_s[c][:, groups].unsqueeze(2).to_broadcast([P, n, GROUP])
            nc.vector.tensor_tensor(grouped(along[c])[:, groups, :], grouped(s[c])[:, groups, :], factor, ALU.mult)

        def finish(c, groups, queue):
            cols = slice(groups.start * GROUP, groups.stop * GROUP)
            result = sb([P, cols.stop - cols.start], F32, "result%d_%d" % (c, groups.start))
            nc.vector.tensor_tensor(result[:], along[c][:, cols], partial[c][:, cols], ALU.add)
            queue.dma_start(out=out[c * P : (c + 1) * P, cols], in_=result[:])

        whole, low, high = slice(0, G), slice(0, G // 2), slice(G // 2, G)
        scale_scores(0, whole)
        scale_scores(1, low)
        finish(0, whole, nc.sync)
        scale_scores(1, high)
        finish(1, low, nc.scalar)
        finish(1, high, nc.sync)
